import numpy as np
import ml_dtypes


def mxq(x, axis, fmt="e4m3"):
    dtype, down = {"e4m3": (ml_dtypes.float8_e4m3fn, 7), "e5m2": (ml_dtypes.float8_e5m2, 14)}[fmt]
    v = np.moveaxis(np.asarray(x, np.float32).astype(ml_dtypes.bfloat16).astype(np.float64), axis, -1)
    blocks = v.reshape(v.shape[:-1] + (-1, 32))
    amax = np.abs(blocks).max(-1, keepdims=True)
    byte = np.maximum(np.where(amax > 0, np.frexp(amax)[1] - 1 + 127, 0) - down, 1)
    scale = np.exp2(byte - 127.0)
    codes = (blocks / scale).astype(np.float32).astype(dtype).astype(np.float64)
    return np.moveaxis((codes * scale).reshape(v.shape), -1, axis)


WIDE = False


def mx_kscale(k):
    if not WIDE:
        return np.ones(k)
    levels = np.array([10, -10, 5, -5, 0])
    if k % 512:
        return np.exp2(np.random.permutation(np.resize(levels, k // 32))).repeat(32)
    a = np.empty((k // 512, 16))
    for p in range(k // 512):
        a[p, :8] = np.random.permutation(np.resize(levels, 8))
        for g in range(8):
            far = levels[np.abs(levels - a[p, g]) >= 10]
            a[p, g + 8] = far[np.random.randint(len(far))]
    return np.exp2(a.ravel()).repeat(32)


def f64(x):
    return np.asarray(x).astype(np.float64)


def striped(idx):
    return np.tile(idx.reshape(-1, 16).T, (8, 1)).astype(np.uint16)


def unstriped(offs):
    return offs[:16].T.reshape(-1).astype(np.int64)


def pack_weight(w):
    k, n = w.shape
    w = f64(np.asarray(w, np.float32).astype(ml_dtypes.bfloat16)).reshape(k // 32, 32, n)
    amax = np.abs(w).max(1)
    byte = np.clip(np.where(amax > 0, np.frexp(amax)[1] - 1 + 127 - 7, 1), 1, 254)
    scaled = (w * np.exp2(127.0 - byte)[:, None, :]).reshape(k, n).astype(np.float32)
    words = np.ascontiguousarray(scaled.reshape(k // 512, 128, 4, n).transpose(0, 1, 3, 2)).astype(ml_dtypes.float8_e4m3fn).view(np.uint8)
    return words, np.ascontiguousarray(byte.astype(np.uint8).reshape(k // 512, 16, n))


def unpack_weight(words, scales):
    g, p, n, _ = words.shape
    vals = np.ascontiguousarray(words).view(ml_dtypes.float8_e4m3fn).astype(np.float64) * np.repeat(np.exp2(scales.astype(np.float64) - 127.0), 8, axis=1)[..., None]
    return vals.transpose(0, 1, 3, 2).reshape(g * 512, n)


K, T, S, N, H = 512, 1024, 512, 256, 512


def setup_inputs():
    n = np.random.standard_normal
    s = mx_kscale(K)[:, None]
    u = mx_kscale(H)
    packed_xT = pack_weight(n((K, T)) * s)
    return {
        "x_words": packed_xT[0],
        "x_scales": packed_xT[1],
        "hT": (n((K, H)) / np.sqrt(K) / s).astype(np.float32),
        "n2": (np.random.uniform(0.5, 1.5, (H, S))).astype(np.float32),
        "bw": (np.random.uniform(0.6, 1.4, (H, S))).astype(np.float32),
        "unit": (np.random.uniform(0.6, 1.4, (H, 1)) * u[:, None]).astype(np.float32),
        "w1": (n((H, N)) / np.sqrt(H) / u[:, None]).astype(np.float32),
        "offs": striped(np.random.permutation(T)[:S]),
        "sib": striped(np.random.permutation(S)),
    }


def reference(x_words, x_scales, hT, n2, bw, unit, w1, offs, sib):
    hTq = mxq(f64(hT), 0, "e4m3")
    xq = unpack_weight(x_words, x_scales)[:, unstriped(offs)]
    y = hTq.T @ xq
    dis = np.log(np.exp(f64(n2) - y) + 1.0)
    ker = f64(bw) / (dis + f64(bw))
    tot = ker.mean(axis=1, keepdims=True)
    wgt = ker / (tot + 0.2)
    ks = ker[:, unstriped(sib)]
    loo = ker - ks
    hid = f64(unit) * (wgt - (0.6 * ((loo) ** 2)))
    return mxq(f64(w1), 0, "e4m3").T @ mxq(hid, 0, "e4m3")

@@ -1,0 +1,259 @@
+from contextlib import ExitStack
+
+import concourse.mybir as mybir
+
+K, T, S, N, H = 512, 1024, 512, 256, 512
+FLOPS = 2 * K * H * S + 2 * H * N * S
+
+F32 = mybir.dt.float32
+BF16 = mybir.dt.bfloat16
+I32 = mybir.dt.int32
+U32 = mybir.dt.uint32
+U16 = mybir.dt.uint16
+U8 = mybir.dt.uint8
+FP8X4 = mybir.dt.float8_e4m3fn_x4
+ALU = mybir.AluOpType
+ACT = mybir.ActivationFunctionType
+
+P = 128
+PACK = 4
+HALF = S // 2
+LIST_GROUP = 16
+OVERLAP = 16
+LINEAR_FROM = 20.0
+HUGE = 2.0**127
+TINY = 2.0**-60
+ORDER = (1, 2, 3, 0)
+CHUNKS = (slice(0, HALF), slice(HALF, S))
+
+
+def tile_picked_ylandk_sqr_p_kernel(
+    tc, x_words, x_scales, hT, n2, bw, unit, w1, offs, sib, out
+):
+    nc = tc.nc
+    with ExitStack() as ctx:
+        keep = ctx.enter_context(tc.tile_pool(name="keep", bufs=1))
+        ring = ctx.enter_context(tc.tile_pool(name="ring", bufs=3))
+        psum = ctx.enter_context(tc.psum_pool(name="psum", bufs=1))
+
+        word_table = keep.tile([P, T], I32, align_bytes=64)
+        scale_table = keep.tile([P, T], U8, align_bytes=64)
+        offs_sb = keep.tile([P, S // LIST_GROUP], U16)
+        sib_sb = keep.tile([P, S // LIST_GROUP], U16)
+        unit_sb = keep.tile([P, PACK], F32)
+        nc.vector.memset(scale_table[:].bitcast(I32), 0)
+        nc.sync.dma_start(out=word_table[:], in_=x_words[0].rearrange("p n t -> p (n t)").bitcast(I32))
+        for q in range(4):
+            nc.sync.dma_start(
+                out=scale_table[32 * q : 32 * q + 4, :].bitcast(I32),
+                in_=x_scales[0, 4 * q : 4 * q + 4, :].bitcast(I32),
+            )
+        nc.sync.dma_start(offs_sb[:], offs)
+        h_rows = hT.rearrange("(p j) c -> p j c", j=PACK)
+        h_raw = [keep.tile([P, PACK, H // 2], F32, name=f"h_raw{u}") for u in range(2)]
+        for u in range(2):
+            nc.sync.dma_start(out=h_raw[u][:], in_=h_rows[:, :, u * (H // 2) : (u + 1) * (H // 2)])
+        n2_rows = n2.rearrange("(p t) c -> p t c", t=PACK)
+        n2_sb = [keep.tile([P, S], F32, name=f"n2_sb{t}") for t in range(PACK)]
+        for t in ORDER:
+            nc.sync.dma_start(out=n2_sb[t][:], in_=n2_rows[:, t, :])
+        bw_rows = bw.rearrange("(p t) c -> p (t c)", t=PACK)
+        bw_sb = keep.tile([P, PACK * S], F32)
+        for u in range(2):
+            cols = slice(2 * u * S, 2 * (u + 1) * S)
+            nc.sync.dma_start(out=bw_sb[:, cols], in_=bw_rows[:, cols])
+        w_raw = keep.tile([P, PACK, N], F32)
+        nc.sync.dma_start(out=w_raw[:], in_=w1.rearrange("(p j) m -> p j m", j=PACK))
+        nc.sync.dma_start(out=unit_sb[:], in_=unit.rearrange("(p t) o -> p (t o)", t=PACK))
+        nc.sync.dma_start(sib_sb[:], sib)
+
+
+        x_codes = keep.tile([P, S], U32, align_bytes=64)
+        x_bytes = keep.tile([P, S], U8, align_bytes=64)
+        nc.vector.tensor_copy(x_bytes[:], scale_table[:].indirect(offs_sb[:]))
+        nc.vector.tensor_copy(x_codes[:], word_table[:].bitcast(U32).indirect(offs_sb[:]))
+
+        h_grouped = keep.tile([P, PACK, P, PACK], BF16, align_bytes=64)
+        for u, copy in enumerate((nc.scalar.copy, nc.vector.tensor_copy)):
+            copy(
+                out=h_grouped[:, :, u * (P // 2) : (u + 1) * (P // 2), :].rearrange("p t m j -> p m t j"),
+                in_=h_raw[u][:].rearrange("p j (m t) -> p m t j", t=PACK),
+            )
+
+        z = keep.tile([P, PACK * S], F32)
+        e = keep.tile([P, PACK * S], F32)
+        z_high = keep.tile([P, PACK * S], F32)
+        for t in ORDER:
+            row = slice(t * S, (t + 1) * S)
+            h_codes = keep.tile([P, P], U32, align_bytes=64, name=f"h_codes{t}")
+            h_bytes = keep.tile([P, P], U8, align_bytes=64, name=f"h_bytes{t}")
+            nc.vector.quantize_mx(
+                out=h_codes[:].bitcast(FP8X4),
+                scales=h_bytes[:],
+                in_=h_grouped[:, t, :, :].rearrange("p m j -> p (m j)"),
+            )
+            y = psum.tile([P, S], F32, name=f"y{t}")
+            nc.tensor.matmul_mx(
+                out=y[:],
+                lhsT=h_codes[:].bitcast(FP8X4),
+                lhsT_scale=h_bytes[:],
+                rhs=x_codes[:].bitcast(FP8X4),
+                rhs_scale=x_bytes[:],
+                start=True,
+                stop=True,
+            )
+            nc.vector.tensor_tensor(out=z[:, row], in0=n2_sb[t][:], in1=y[:], op=ALU.subtract)
+            nc.scalar.activation(out=e[:, row], in_=z[:, row], func=ACT.Sigmoid, scale=-1.0)
+            nc.gpsimd.tensor_scalar(
+                out=z_high[:, row], in0=z[:, row], scalar1=HUGE, scalar2=LINEAR_FROM, op0=ALU.min, op1=ALU.max
+            )
+
+        w_grouped = keep.tile([P, N, PACK], BF16, align_bytes=64)
+        nc.vector.tensor_copy(
+            out=w_grouped[:].rearrange("p (c i) j -> p c j i", i=4),
+            in_=w_raw[:].rearrange("p j (c i) -> p c j i", i=4),
+        )
+        w_codes = keep.tile([P, N], U32, align_bytes=64)
+        w_bytes = keep.tile([P, N], U8, align_bytes=64)
+        nc.vector.quantize_mx(
+            out=w_codes[:].bitcast(FP8X4), scales=w_bytes[:], in_=w_grouped[:].rearrange("p c j -> p (c j)")
+        )
+
+        loo_gain = keep.tile([P, PACK], F32)
+        nc.vector.tensor_scalar(out=loo_gain[:], in0=unit_sb[:], scalar1=0.6, scalar2=None, op0=ALU.mult)
+
+        bw_plus = keep.tile([P, PACK * S], F32)
+        for t in (0,) + ORDER[:-1]:
+            row = slice(t * S, (t + 1) * S)
+            nc.vector.scalar_tensor_tensor(
+                out=bw_plus[:, row], in0=z_high[:, row], scalar=LINEAR_FROM, in1=bw_sb[:, row],
+                op0=ALU.subtract, op1=ALU.add,
+            )
+        tiny = keep.tile([P, 1], F32)
+        nc.vector.memset(tiny[:], TINY)
+        pieces = (slice(S - OVERLAP, 2 * S), slice(2 * S, 3 * S), slice(3 * S, 4 * S), slice(0, S - OVERLAP))
+        first_log = keep.tile([P, S + OVERLAP], F32)
+        homes = (first_log[:], e[:, S : 2 * S], e[:, 2 * S : 3 * S], e[:, 3 * S : 4 * S - OVERLAP])
+        den = keep.tile([P, PACK * S], F32)
+        den_sq = keep.tile([P, PACK * S], F32)
+        for n, (piece, soft) in enumerate(zip(pieces, homes)):
+            nc.scalar.activation(out=soft, in_=e[:, piece], func=ACT.Ln, bias=tiny[:])
+            nc.vector.scalar_tensor_tensor(
+                out=den[:, piece], in0=soft, scalar=-LINEAR_FROM, in1=bw_plus[:, piece], op0=ALU.max, op1=ALU.subtract
+            )
+            if n > 0:
+                before = pieces[n - 1]
+                nc.vector.tensor_tensor(out=den_sq[:, before], in0=den[:, before], in1=den[:, before], op=ALU.mult)
+
+        ker = [keep.tile([P, S], F32, name=f"ker{t}") for t in range(PACK)]
+        ker_sib = [keep.tile([P, S], F32, name=f"ker_sib{t}") for t in range(PACK)]
+        loo = [keep.tile([P, S], F32, name=f"loo{t}") for t in range(PACK)]
+        penalty = [keep.tile([P, S], F32, name=f"penalty{t}") for t in range(PACK)]
+        row_sum = keep.tile([P, PACK], F32)
+        ker_gain = keep.tile([P, PACK], F32)
+        hid = [keep.tile([P, PACK, c.stop - c.start], BF16, name=f"hid{c.start}") for c in CHUNKS]
+        inv_home = {ORDER[0]: e[:, 0:S]}
+        for before, t in zip(ORDER, ORDER[1:]):
+            inv_home[t] = den_sq[:, before * S : (before + 1) * S]
+        out_rows = out.rearrange("(b p) c -> p b c", p=P)
+
+        def reciprocal_row(t):
+            row = slice(t * S, (t + 1) * S)
+            if t == ORDER[-1]:
+                nc.scalar.activation(out=den_sq[:, pieces[-1]], in_=den[:, pieces[-1]], func=ACT.Square)
+            nc.scalar.activation(out=inv_home[t], in_=den_sq[:, row], func=ACT.Abs_reciprocal_sqrt)
+
+        def kernel_row(t):
+            row = slice(t * S, (t + 1) * S)
+            nc.vector.scalar_tensor_tensor(
+                out=ker[t][:], in0=inv_home[t], scalar=1.0, in1=bw_sb[:, row], op0=ALU.mult, op1=ALU.mult,
+                accum_out=row_sum[:, t : t + 1],
+            )
+
+        def gains(cols):
+            width = cols.stop - cols.start
+            shifted = ring.tile([P, width], F32)
+            nc.vector.tensor_scalar(
+                out=shifted[:], in0=row_sum[:, cols], scalar1=1.0 / S, scalar2=0.2, op0=ALU.mult, op1=ALU.add
+            )
+            inverse = ring.tile([P, width], F32)
+            nc.vector.reciprocal(out=inverse[:], in_=shifted[:])
+            nc.vector.tensor_tensor(out=ker_gain[:, cols], in0=inverse[:], in1=unit_sb[:, cols], op=ALU.mult)
+
+        def fetch(t, cols):
+            entries = slice(cols.start // LIST_GROUP, cols.stop // LIST_GROUP)
+            nc.scalar.activation(out=ker_sib[t][:, cols], in_=ker[t][:].indirect(sib_sb[:, entries]), func=ACT.Copy)
+
+        def difference(t, cols):
+            nc.vector.tensor_tensor(out=loo[t][:, cols], in0=ker[t][:, cols], in1=ker_sib[t][:, cols], op=ALU.subtract)
+
+        def square(t, cols):
+            nc.vector.scalar_tensor_tensor(
+                out=penalty[t][:, cols], in0=loo[t][:, cols], scalar=loo_gain[:, t : t + 1], in1=loo[t][:, cols],
+                op0=ALU.mult, op1=ALU.mult,
+            )
+
+        def hidden(t, n):
+            cols = CHUNKS[n]
+            nc.vector.scalar_tensor_tensor(
+                out=hid[n][:, t, :], in0=ker[t][:, cols], scalar=ker_gain[:, t : t + 1], in1=penalty[t][:, cols],
+                op0=ALU.mult, op1=ALU.subtract,
+            )
+
+        def readout(n, group_copy, out_copy):
+            cols = CHUNKS[n]
+            width = cols.stop - cols.start
+            hid_grouped = keep.tile([P, width, PACK], BF16, align_bytes=64, name=f"hid_grouped{n}")
+            group_copy(
+                out=hid_grouped[:].rearrange("p (c i) t -> p c t i", i=4),
+                in_=hid[n][:].rearrange("p t (c i) -> p c t i", i=4),
+            )
+            hid_codes = keep.tile([P, width], U32, align_bytes=64, name=f"hid_codes{n}")
+            hid_bytes = keep.tile([P, width], U8, align_bytes=64, name=f"hid_bytes{n}")
+            nc.vector.quantize_mx(
+                out=hid_codes[:].bitcast(FP8X4), scales=hid_bytes[:],
+                in_=hid_grouped[:].rearrange("p c t -> p (c t)"),
+            )
+            result = keep.tile([P, N // P, width], F32, name=f"result{n}")
+            for b in range(N // P):
+                acc = psum.tile([P, width], F32, name=f"acc{n}_{b}")
+                nc.tensor.matmul_mx(
+                    out=acc[:],
+                    lhsT=w_codes[:, b * P : (b + 1) * P].bitcast(FP8X4),
+                    lhsT_scale=w_bytes[:, b * P : (b + 1) * P],
+                    rhs=hid_codes[:].bitcast(FP8X4),
+                    rhs_scale=hid_bytes[:],
+                    start=True,
+                    stop=True,
+                )
+                out_copy[b](out=result[:, b, :], in_=acc[:])
+            nc.sync.dma_start(out=out_rows[:, :, cols], in_=result[:])
+
+        whole = slice(0, S)
+        first, second, third, last = ORDER
+        reciprocal_row(first)
+        kernel_row(first)
+        reciprocal_row(second)
+        kernel_row(second)
+        gains(slice(first, second + 1))
+        for t, following in ((first, third), (second, last), (third, None)):
+            for cols in CHUNKS:
+                fetch(t, cols)
+            if following is not None:
+                reciprocal_row(following)
+            difference(t, whole)
+            if following is not None:
+                kernel_row(following)
+            square(t, whole)
+            if following is not None:
+                gains(slice(following, following + 1))
+            for n in range(len(CHUNKS)):
+                hidden(t, n)
+        for cols in CHUNKS:
+            fetch(last, cols)
+        for n, cols in enumerate(CHUNKS):
+            difference(last, cols)
+            square(last, cols)
+            hidden(last, n)
+        readout(0, nc.scalar.copy, (nc.scalar.copy, nc.scalar.copy))
+        readout(1, nc.vector.tensor_copy, (nc.scalar.copy, nc.vector.tensor_copy))

@@ -19,12 +19,14 @@ P = 128
 PACK = 4
 HALF = S // 2
 LIST_GROUP = 16
-OVERLAP = 16
 LINEAR_FROM = 20.0
 HUGE = 2.0**127
 TINY = 2.0**-60
-ORDER = (1, 2, 3, 0)
-CHUNKS = (slice(0, HALF), slice(HALF, S))
+ORDER = (0, 1, 2, 3)
+CHUNKS = (slice(0, 256), slice(256, 384), slice(384, 512))
+HALVES = (slice(0, HALF), slice(HALF, S))
+SPLIT = 24
+VECTOR_SQUARES = 2
 
 
 def tile_picked_ylandk_sqr_p_kernel(
@@ -35,13 +37,14 @@ def tile_picked_ylandk_sqr_p_kernel(
         keep = ctx.enter_context(tc.tile_pool(name="keep", bufs=1))
         ring = ctx.enter_context(tc.tile_pool(name="ring", bufs=3))
         psum = ctx.enter_context(tc.psum_pool(name="psum", bufs=1))
+        first, second, third, last = ORDER
 
         word_table = keep.tile([P, T], I32, align_bytes=64)
         scale_table = keep.tile([P, T], U8, align_bytes=64)
         offs_sb = keep.tile([P, S // LIST_GROUP], U16)
         sib_sb = keep.tile([P, S // LIST_GROUP], U16)
         unit_sb = keep.tile([P, PACK], F32)
-        nc.vector.memset(scale_table[:].bitcast(I32), 0)
+        nc.gpsimd.memset(scale_table[:].bitcast(I32), 0)
         nc.sync.dma_start(out=word_table[:], in_=x_words[0].rearrange("p n t -> p (n t)").bitcast(I32))
         for q in range(4):
             nc.sync.dma_start(
@@ -54,37 +57,44 @@ def tile_picked_ylandk_sqr_p_kernel(
         for u in range(2):
             nc.sync.dma_start(out=h_raw[u][:], in_=h_rows[:, :, u * (H // 2) : (u + 1) * (H // 2)])
         n2_rows = n2.rearrange("(p t) c -> p t c", t=PACK)
-        n2_sb = [keep.tile([P, S], F32, name=f"n2_sb{t}") for t in range(PACK)]
+        n2_sb = [keep.tile([P, S], F32, name=f"n2_sb{t}", align_bytes=64) for t in range(PACK)]
         for t in ORDER:
             nc.sync.dma_start(out=n2_sb[t][:], in_=n2_rows[:, t, :])
+        w_raw = keep.tile([P, PACK, N], F32)
+        nc.sync.dma_start(out=w_raw[:], in_=w1.rearrange("(p j) m -> p j m", j=PACK))
         bw_rows = bw.rearrange("(p t) c -> p (t c)", t=PACK)
         bw_sb = keep.tile([P, PACK * S], F32)
         for u in range(2):
             cols = slice(2 * u * S, 2 * (u + 1) * S)
             nc.sync.dma_start(out=bw_sb[:, cols], in_=bw_rows[:, cols])
-        w_raw = keep.tile([P, PACK, N], F32)
-        nc.sync.dma_start(out=w_raw[:], in_=w1.rearrange("(p j) m -> p j m", j=PACK))
         nc.sync.dma_start(out=unit_sb[:], in_=unit.rearrange("(p t) o -> p (t o)", t=PACK))
         nc.sync.dma_start(sib_sb[:], sib)
 
-
         x_codes = keep.tile([P, S], U32, align_bytes=64)
         x_bytes = keep.tile([P, S], U8, align_bytes=64)
-        nc.vector.tensor_copy(x_bytes[:], scale_table[:].indirect(offs_sb[:]))
         nc.vector.tensor_copy(x_codes[:], word_table[:].bitcast(U32).indirect(offs_sb[:]))
+        nc.vector.tensor_copy(x_bytes[:], scale_table[:].indirect(offs_sb[:]))
 
         h_grouped = keep.tile([P, PACK, P, PACK], BF16, align_bytes=64)
-        for u, copy in enumerate((nc.scalar.copy, nc.vector.tensor_copy)):
+        for u, lo, hi, copy in (
+            (0, 0, 64, nc.scalar.copy),
+            (1, 0, SPLIT, nc.scalar.copy),
+            (1, SPLIT, 64, nc.vector.tensor_copy),
+        ):
             copy(
-                out=h_grouped[:, :, u * (P // 2) : (u + 1) * (P // 2), :].rearrange("p t m j -> p m t j"),
-                in_=h_raw[u][:].rearrange("p j (m t) -> p m t j", t=PACK),
+                out=h_grouped[:, :, 64 * u + lo : 64 * u + hi, :].rearrange("p t m j -> p m t j"),
+                in_=h_raw[u][:, :, PACK * lo : PACK * hi].rearrange("p j (m t) -> p m t j", t=PACK),
             )
 
-        z = keep.tile([P, PACK * S], F32)
-        e = keep.tile([P, PACK * S], F32)
+        z_yard = keep.tile([P, 2 * S], F32)
+        sig_yard = keep.tile([P, 2 * S], F32)
+        middle = slice(HALF, HALF + S)
+        z = {t: keep.tile([P, S], F32, name=f"z{t}")[:] for t in ORDER[:-1]}
+        sig = {t: keep.tile([P, S], F32, name=f"sig{t}")[:] for t in ORDER[:-1]}
+        z[last] = z_yard[:, middle]
+        sig[last] = sig_yard[:, middle]
         z_high = keep.tile([P, PACK * S], F32)
         for t in ORDER:
-            row = slice(t * S, (t + 1) * S)
             h_codes = keep.tile([P, P], U32, align_bytes=64, name=f"h_codes{t}")
             h_bytes = keep.tile([P, P], U8, align_bytes=64, name=f"h_bytes{t}")
             nc.vector.quantize_mx(
@@ -102,48 +112,47 @@ def tile_picked_ylandk_sqr_p_kernel(
                 start=True,
                 stop=True,
             )
-            nc.vector.tensor_tensor(out=z[:, row], in0=n2_sb[t][:], in1=y[:], op=ALU.subtract)
-            nc.scalar.activation(out=e[:, row], in_=z[:, row], func=ACT.Sigmoid, scale=-1.0)
-            nc.gpsimd.tensor_scalar(
-                out=z_high[:, row], in0=z[:, row], scalar1=HUGE, scalar2=LINEAR_FROM, op0=ALU.min, op1=ALU.max
+            nc.vector.tensor_tensor(out=z[t], in0=n2_sb[t][:], in1=y[:], op=ALU.subtract)
+            nc.scalar.activation(out=sig[t], in_=z[t], func=ACT.Sigmoid, scale=-1.0)
+            engine = nc.gpsimd
+            engine.tensor_scalar(
+                out=z_high[:, t * S : (t + 1) * S], in0=z[t], scalar1=HUGE, scalar2=LINEAR_FROM,
+                op0=ALU.min, op1=ALU.max,
             )
 
-        w_grouped = keep.tile([P, N, PACK], BF16, align_bytes=64)
+        w_grouped = keep.tile([P, N, PACK], BF16, align_bytes=64, name=f"n2_sb{last}")
         nc.vector.tensor_copy(
             out=w_grouped[:].rearrange("p (c i) j -> p c j i", i=4),
             in_=w_raw[:].rearrange("p j (c i) -> p c j i", i=4),
         )
+        bw_plus = keep.tile([P, PACK * S], F32)
         w_codes = keep.tile([P, N], U32, align_bytes=64)
         w_bytes = keep.tile([P, N], U8, align_bytes=64)
+        for u in range(2):
+            cols = slice(2 * u * S, 2 * (u + 1) * S)
+            nc.vector.scalar_tensor_tensor(
+                out=bw_plus[:, cols], in0=z_high[:, cols], scalar=LINEAR_FROM, in1=bw_sb[:, cols],
+                op0=ALU.subtract, op1=ALU.add,
+            )
         nc.vector.quantize_mx(
             out=w_codes[:].bitcast(FP8X4), scales=w_bytes[:], in_=w_grouped[:].rearrange("p c j -> p (c j)")
         )
-
         loo_gain = keep.tile([P, PACK], F32)
-        nc.vector.tensor_scalar(out=loo_gain[:], in0=unit_sb[:], scalar1=0.6, scalar2=None, op0=ALU.mult)
-
-        bw_plus = keep.tile([P, PACK * S], F32)
-        for t in (0,) + ORDER[:-1]:
-            row = slice(t * S, (t + 1) * S)
-            nc.vector.scalar_tensor_tensor(
-                out=bw_plus[:, row], in0=z_high[:, row], scalar=LINEAR_FROM, in1=bw_sb[:, row],
-                op0=ALU.subtract, op1=ALU.add,
-            )
+        nc.gpsimd.tensor_scalar(out=loo_gain[:], in0=unit_sb[:], scalar1=-0.6, scalar2=0.0, op0=ALU.mult, op1=ALU.add)
         tiny = keep.tile([P, 1], F32)
-        nc.vector.memset(tiny[:], TINY)
-        pieces = (slice(S - OVERLAP, 2 * S), slice(2 * S, 3 * S), slice(3 * S, 4 * S), slice(0, S - OVERLAP))
-        first_log = keep.tile([P, S + OVERLAP], F32)
-        homes = (first_log[:], e[:, S : 2 * S], e[:, 2 * S : 3 * S], e[:, 3 * S : 4 * S - OVERLAP])
-        den = keep.tile([P, PACK * S], F32)
-        den_sq = keep.tile([P, PACK * S], F32)
-        for n, (piece, soft) in enumerate(zip(pieces, homes)):
-            nc.scalar.activation(out=soft, in_=e[:, piece], func=ACT.Ln, bias=tiny[:])
+        nc.gpsimd.memset(tiny[:], TINY)
+
+        log_home = {first: z_yard[:, 0:S], second: z_yard[:, S : 2 * S], third: sig[first], last: sig[second]}
+        den = [keep.tile([P, S], F32, name=f"den{t}") for t in range(PACK)]
+        den_sq = [keep.tile([P, S], F32, name=f"den_sq{t}") for t in range(2)] * 2
+        for t in ORDER:
+            nc.scalar.activation(out=log_home[t], in_=sig[t], func=ACT.Ln, bias=tiny[:])
             nc.vector.scalar_tensor_tensor(
-                out=den[:, piece], in0=soft, scalar=-LINEAR_FROM, in1=bw_plus[:, piece], op0=ALU.max, op1=ALU.subtract
+                out=den[t][:], in0=log_home[t], scalar=-LINEAR_FROM, in1=bw_plus[:, t * S : (t + 1) * S],
+                op0=ALU.max, op1=ALU.subtract,
             )
-            if n > 0:
-                before = pieces[n - 1]
-                nc.vector.tensor_tensor(out=den_sq[:, before], in0=den[:, before], in1=den[:, before], op=ALU.mult)
+            if t < 2:
+                nc.vector.tensor_tensor(out=den_sq[t][:], in0=den[t][:], in1=den[t][:], op=ALU.mult)
 
         ker = [keep.tile([P, S], F32, name=f"ker{t}") for t in range(PACK)]
         ker_sib = [keep.tile([P, S], F32, name=f"ker_sib{t}") for t in range(PACK)]
@@ -151,23 +160,24 @@ def tile_picked_ylandk_sqr_p_kernel(
         penalty = [keep.tile([P, S], F32, name=f"penalty{t}") for t in range(PACK)]
         row_sum = keep.tile([P, PACK], F32)
         ker_gain = keep.tile([P, PACK], F32)
-        hid = [keep.tile([P, PACK, c.stop - c.start], BF16, name=f"hid{c.start}") for c in CHUNKS]
-        inv_home = {ORDER[0]: e[:, 0:S]}
-        for before, t in zip(ORDER, ORDER[1:]):
-            inv_home[t] = den_sq[:, before * S : (before + 1) * S]
+        hid = [keep.tile([P, PACK, HALF], BF16, name=f"hid{h}") for h in range(2)]
+        inv_home = {first: sig_yard[:, 0:S], second: sig_yard[:, S : 2 * S], third: den[first][:], last: den[second][:]}
         out_rows = out.rearrange("(b p) c -> p b c", p=P)
+        weighted = {t: keep.tile([P, S], F32, name=f"weighted{t}") for t in ORDER[2:]}
 
         def reciprocal_row(t):
-            row = slice(t * S, (t + 1) * S)
-            if t == ORDER[-1]:
-                nc.scalar.activation(out=den_sq[:, pieces[-1]], in_=den[:, pieces[-1]], func=ACT.Square)
-            nc.scalar.activation(out=inv_home[t], in_=den_sq[:, row], func=ACT.Abs_reciprocal_sqrt)
+            nc.scalar.activation(out=inv_home[t], in_=den_sq[t][:], func=ACT.Abs_reciprocal_sqrt)
+
+        def vector_den_square(t):
+            nc.vector.tensor_tensor(out=den_sq[t][:], in0=den[t][:], in1=den[t][:], op=ALU.mult)
+
+        def scalar_den_square(t):
+            nc.scalar.activation(out=den_sq[t][:], in_=den[t][:], func=ACT.Square)
 
         def kernel_row(t):
-            row = slice(t * S, (t + 1) * S)
             nc.vector.scalar_tensor_tensor(
-                out=ker[t][:], in0=inv_home[t], scalar=1.0, in1=bw_sb[:, row], op0=ALU.mult, op1=ALU.mult,
-                accum_out=row_sum[:, t : t + 1],
+                out=ker[t][:], in0=inv_home[t], scalar=1.0, in1=bw_sb[:, t * S : (t + 1) * S],
+                op0=ALU.mult, op1=ALU.mult, accum_out=row_sum[:, t : t + 1],
             )
 
         def gains(cols):
@@ -187,26 +197,37 @@ def tile_picked_ylandk_sqr_p_kernel(
         def difference(t, cols):
             nc.vector.tensor_tensor(out=loo[t][:, cols], in0=ker[t][:, cols], in1=ker_sib[t][:, cols], op=ALU.subtract)
 
-        def square(t, cols):
-            nc.vector.scalar_tensor_tensor(
-                out=penalty[t][:, cols], in0=loo[t][:, cols], scalar=loo_gain[:, t : t + 1], in1=loo[t][:, cols],
-                op0=ALU.mult, op1=ALU.mult,
-            )
+        def weigh(t):
+            nc.scalar.activation(out=weighted[t][:], in_=ker[t][:], func=ACT.Copy, scale=ker_gain[:, t : t + 1])
 
-        def hidden(t, n):
-            cols = CHUNKS[n]
+        def square(t, cols):
+            if t in weighted:
+                nc.scalar.activation(out=penalty[t][:, cols], in_=loo[t][:, cols], func=ACT.Square)
+            else:
+                nc.vector.scalar_tensor_tensor(
+                    out=penalty[t][:, cols], in0=loo[t][:, cols], scalar=loo_gain[:, t : t + 1], in1=loo[t][:, cols],
+                    op0=ALU.mult, op1=ALU.mult,
+                )
+
+        def hidden(t, cols):
+            h, lo = divmod(cols.start, HALF)
+            if t in weighted:
+                scaled, gain, plain = penalty[t], loo_gain, weighted[t]
+            else:
+                scaled, gain, plain = ker[t], ker_gain, penalty[t]
             nc.vector.scalar_tensor_tensor(
-                out=hid[n][:, t, :], in0=ker[t][:, cols], scalar=ker_gain[:, t : t + 1], in1=penalty[t][:, cols],
-                op0=ALU.mult, op1=ALU.subtract,
+                out=hid[h][:, t, lo : lo + cols.stop - cols.start], in0=scaled[:, cols], scalar=gain[:, t : t + 1], in1=plain[:, cols],
+                op0=ALU.mult, op1=ALU.add,
             )
 
         def readout(n, group_copy, out_copy):
             cols = CHUNKS[n]
             width = cols.stop - cols.start
+            h, lo = divmod(cols.start, HALF)
             hid_grouped = keep.tile([P, width, PACK], BF16, align_bytes=64, name=f"hid_grouped{n}")
             group_copy(
                 out=hid_grouped[:].rearrange("p (c i) t -> p c t i", i=4),
-                in_=hid[n][:].rearrange("p t (c i) -> p c t i", i=4),
+                in_=hid[h][:, :, lo : lo + width].rearrange("p t (c i) -> p c t i", i=4),
             )
             hid_codes = keep.tile([P, width], U32, align_bytes=64, name=f"hid_codes{n}")
             hid_bytes = keep.tile([P, width], U8, align_bytes=64, name=f"hid_bytes{n}")
@@ -214,11 +235,10 @@ def tile_picked_ylandk_sqr_p_kernel(
                 out=hid_codes[:].bitcast(FP8X4), scales=hid_bytes[:],
                 in_=hid_grouped[:].rearrange("p c t -> p (c t)"),
             )
-            result = keep.tile([P, N // P, width], F32, name=f"result{n}")
+            acc = psum.tile([P, N // P, width], F32, name=f"acc{n}")
             for b in range(N // P):
-                acc = psum.tile([P, width], F32, name=f"acc{n}_{b}")
                 nc.tensor.matmul_mx(
-                    out=acc[:],
+                    out=acc[:, b, :],
                     lhsT=w_codes[:, b * P : (b + 1) * P].bitcast(FP8X4),
                     lhsT_scale=w_bytes[:, b * P : (b + 1) * P],
                     rhs=hid_codes[:].bitcast(FP8X4),
@@ -226,34 +246,49 @@ def tile_picked_ylandk_sqr_p_kernel(
                     start=True,
                     stop=True,
                 )
-                out_copy[b](out=result[:, b, :], in_=acc[:])
+            result = keep.tile([P, N // P, width], F32, name=f"result{n}")
+            out_copy(out=result[:], in_=acc[:])
             nc.sync.dma_start(out=out_rows[:, :, cols], in_=result[:])
 
         whole = slice(0, S)
-        first, second, third, last = ORDER
+        left, right = HALVES
         reciprocal_row(first)
-        kernel_row(first)
         reciprocal_row(second)
+        kernel_row(first)
+        fetch(first, left)
         kernel_row(second)
-        gains(slice(first, second + 1))
-        for t, following in ((first, third), (second, last), (third, None)):
-            for cols in CHUNKS:
+        vector_den_square(third)
+        fetch(first, right)
+        reciprocal_row(third)
+        scalar_den_square(last)
+        difference(first, whole)
+        kernel_row(third)
+        fetch(second, left)
+        reciprocal_row(last)
+        fetch(second, right)
+        square(first, whole)
+        kernel_row(last)
+        difference(second, whole)
+        for t in (third, last):
+            for cols in HALVES:
                 fetch(t, cols)
-            if following is not None:
-                reciprocal_row(following)
-            difference(t, whole)
-            if following is not None:
-                kernel_row(following)
-            square(t, whole)
-            if following is not None:
-                gains(slice(following, following + 1))
-            for n in range(len(CHUNKS)):
-                hidden(t, n)
-        for cols in CHUNKS:
-            fetch(last, cols)
-        for n, cols in enumerate(CHUNKS):
-            difference(last, cols)
-            square(last, cols)
-            hidden(last, n)
-        readout(0, nc.scalar.copy, (nc.scalar.copy, nc.scalar.copy))
-        readout(1, nc.vector.tensor_copy, (nc.scalar.copy, nc.vector.tensor_copy))
+        gains(slice(first, last + 1))
+        square(second, whole)
+        difference(third, whole)
+        difference(last, whole)
+        for t in weighted:
+            weigh(t)
+        for cols in HALVES:
+            for t in (third, last):
+                square(t, cols)
+        for t in (first, second):
+            for cols in HALVES:
+                hidden(t, cols)
+        for t in (third, last):
+            hidden(t, left)
+        readout(0, nc.vector.tensor_copy, nc.scalar.copy)
+        hidden(third, right)
+        for cols in CHUNKS[1:]:
+            hidden(last, cols)
+        for n in range(1, len(CHUNKS)):
+            readout(n, (nc.scalar.copy, nc.vector.tensor_copy)[n - 1], (nc.scalar.copy, nc.vector.tensor_copy)[n - 1])

@@ -20,13 +20,12 @@ PACK = 4
 HALF = S // 2
 LIST_GROUP = 16
 LINEAR_FROM = 20.0
-HUGE = 2.0**127
-TINY = 2.0**-60
-ORDER = (0, 1, 2, 3)
+MEAN_SHIFT = 0.2
+LOO_WEIGHT = 0.6
+FLOOR = 2.0**-100
+SCALAR_SHARE = 24
 CHUNKS = (slice(0, 256), slice(256, 384), slice(384, 512))
-HALVES = (slice(0, HALF), slice(HALF, S))
-SPLIT = 24
-VECTOR_SQUARES = 2
+EARLY, LATE = slice(0, 2), slice(2, 4)
 
 
 def tile_picked_ylandk_sqr_p_kernel(
@@ -35,9 +34,10 @@ def tile_picked_ylandk_sqr_p_kernel(
     nc = tc.nc
     with ExitStack() as ctx:
         keep = ctx.enter_context(tc.tile_pool(name="keep", bufs=1))
-        ring = ctx.enter_context(tc.tile_pool(name="ring", bufs=3))
         psum = ctx.enter_context(tc.psum_pool(name="psum", bufs=1))
-        first, second, third, last = ORDER
+
+        def flat(t, cols=slice(0, S)):
+            return slice(t * S + cols.start, t * S + cols.stop)
 
         word_table = keep.tile([P, T], I32, align_bytes=64)
         scale_table = keep.tile([P, T], U8, align_bytes=64)
@@ -56,19 +56,25 @@ def tile_picked_ylandk_sqr_p_kernel(
         h_raw = [keep.tile([P, PACK, H // 2], F32, name=f"h_raw{u}") for u in range(2)]
         for u in range(2):
             nc.sync.dma_start(out=h_raw[u][:], in_=h_rows[:, :, u * (H // 2) : (u + 1) * (H // 2)])
-        n2_rows = n2.rearrange("(p t) c -> p t c", t=PACK)
-        n2_sb = [keep.tile([P, S], F32, name=f"n2_sb{t}", align_bytes=64) for t in range(PACK)]
-        for t in ORDER:
-            nc.sync.dma_start(out=n2_sb[t][:], in_=n2_rows[:, t, :])
+        nc.sync.dma_start(out=unit_sb[:], in_=unit.rearrange("(p t) o -> p (t o)", t=PACK))
+        n2_rows = n2.rearrange("(p t) c -> p (t c)", t=PACK)
+        n2_yard = keep.tile([P, 2 * S - HALF + PACK * S], F32)
+        n2_sb = n2_yard[:, 2 * S - HALF :]
         w_raw = keep.tile([P, PACK, N], F32)
         nc.sync.dma_start(out=w_raw[:], in_=w1.rearrange("(p j) m -> p j m", j=PACK))
+        for t in (1, 2, 3, 0):
+            nc.sync.dma_start(out=n2_sb[:, flat(t)], in_=n2_rows[:, flat(t)])
         bw_rows = bw.rearrange("(p t) c -> p (t c)", t=PACK)
         bw_sb = keep.tile([P, PACK * S], F32)
-        for u in range(2):
-            cols = slice(2 * u * S, 2 * (u + 1) * S)
+        pairs = (slice(0, 2 * S), slice(2 * S, 4 * S))
+        for cols in reversed(pairs):
             nc.sync.dma_start(out=bw_sb[:, cols], in_=bw_rows[:, cols])
-        nc.sync.dma_start(out=unit_sb[:], in_=unit.rearrange("(p t) o -> p (t o)", t=PACK))
         nc.sync.dma_start(sib_sb[:], sib)
+
+        unshift = keep.tile([P, 1], F32)
+        nc.gpsimd.memset(unshift[:], -LINEAR_FROM)
+        tiny = keep.tile([P, 1], F32)
+        nc.scalar.activation(out=tiny[:], in_=unshift[:], func=ACT.Sigmoid, scale=2.0)
 
         x_codes = keep.tile([P, S], U32, align_bytes=64)
         x_bytes = keep.tile([P, S], U8, align_bytes=64)
@@ -77,218 +83,245 @@ def tile_picked_ylandk_sqr_p_kernel(
 
         h_grouped = keep.tile([P, PACK, P, PACK], BF16, align_bytes=64)
         for u, lo, hi, copy in (
-            (0, 0, 64, nc.scalar.copy),
-            (1, 0, SPLIT, nc.scalar.copy),
-            (1, SPLIT, 64, nc.vector.tensor_copy),
+            (0, 0, P // 2, nc.scalar.copy),
+            (1, 0, SCALAR_SHARE, nc.scalar.copy),
+            (1, SCALAR_SHARE, P // 2, nc.vector.tensor_copy),
         ):
             copy(
                 out=h_grouped[:, :, 64 * u + lo : 64 * u + hi, :].rearrange("p t m j -> p m t j"),
                 in_=h_raw[u][:, :, PACK * lo : PACK * hi].rearrange("p j (m t) -> p m t j", t=PACK),
             )
 
-        z_yard = keep.tile([P, 2 * S], F32)
-        sig_yard = keep.tile([P, 2 * S], F32)
-        middle = slice(HALF, HALF + S)
-        z = {t: keep.tile([P, S], F32, name=f"z{t}")[:] for t in ORDER[:-1]}
-        sig = {t: keep.tile([P, S], F32, name=f"sig{t}")[:] for t in ORDER[:-1]}
-        z[last] = z_yard[:, middle]
-        sig[last] = sig_yard[:, middle]
-        z_high = keep.tile([P, PACK * S], F32)
-        for t in ORDER:
-            h_codes = keep.tile([P, P], U32, align_bytes=64, name=f"h_codes{t}")
-            h_bytes = keep.tile([P, P], U8, align_bytes=64, name=f"h_bytes{t}")
+        unit_sign = keep.tile([P, PACK], F32)
+        nc.scalar.activation(out=unit_sign[:], in_=unit_sb[:], func=ACT.Sign)
+        unit_size = keep.tile([P, PACK], F32)
+        nc.scalar.activation(out=unit_size[:], in_=unit_sb[:], func=ACT.Abs, scale=1.0 / MEAN_SHIFT)
+        w_signed = keep.tile([P, PACK, N], BF16)
+        for j in range(PACK):
+            nc.scalar.activation(out=w_signed[:, j, :], in_=w_raw[:, j, :], func=ACT.Copy, scale=unit_sign[:, j : j + 1])
+
+        shifted = keep.tile([P, PACK * S], F32, align_bytes=64)
+        cut = HALF + HALF // 2
+        sig_yard = keep.tile([P, S - cut + PACK * S], F32)
+        sig = sig_yard[:, S - cut :]
+        left, right, whole = slice(0, HALF), slice(HALF, S), slice(0, S)
+        h_codes = keep.tile([P, PACK, P], U32, align_bytes=64)
+        h_bytes = keep.tile([P, PACK, P], U8, align_bytes=64)
+        for t in (1, 2, 3, 0):
             nc.vector.quantize_mx(
-                out=h_codes[:].bitcast(FP8X4),
-                scales=h_bytes[:],
+                out=h_codes[:, t, :].bitcast(FP8X4),
+                scales=h_bytes[:, t, :],
                 in_=h_grouped[:, t, :, :].rearrange("p m j -> p (m j)"),
             )
-            y = psum.tile([P, S], F32, name=f"y{t}")
+        pieces = ((1, left), (1, right), (2, whole), (3, whole), (0, left), (0, right))
+        for bank, (t, cols) in enumerate(pieces):
+            y = psum.tile([P, cols.stop - cols.start], F32, name=f"y{bank}", tag=f"bank{bank}")
             nc.tensor.matmul_mx(
                 out=y[:],
-                lhsT=h_codes[:].bitcast(FP8X4),
-                lhsT_scale=h_bytes[:],
-                rhs=x_codes[:].bitcast(FP8X4),
-                rhs_scale=x_bytes[:],
+                lhsT=h_codes[:, t, :].bitcast(FP8X4),
+                lhsT_scale=h_bytes[:, t, :],
+                rhs=x_codes[:, cols].bitcast(FP8X4),
+                rhs_scale=x_bytes[:, cols],
                 start=True,
                 stop=True,
             )
-            nc.vector.tensor_tensor(out=z[t], in0=n2_sb[t][:], in1=y[:], op=ALU.subtract)
-            nc.scalar.activation(out=sig[t], in_=z[t], func=ACT.Sigmoid, scale=-1.0)
-            engine = nc.gpsimd
-            engine.tensor_scalar(
-                out=z_high[:, t * S : (t + 1) * S], in0=z[t], scalar1=HUGE, scalar2=LINEAR_FROM,
-                op0=ALU.min, op1=ALU.max,
+            at = flat(t, cols)
+            nc.vector.scalar_tensor_tensor(
+                out=shifted[:, at], in0=y[:], scalar=LINEAR_FROM, in1=n2_sb[:, at], op0=ALU.add, op1=ALU.subtract
+            )
+            nc.scalar.activation(out=sig[:, at], in_=shifted[:, at], func=ACT.Sigmoid, bias=unshift[:])
+
+        linear = (n2_sb[:, pairs[1]], n2_yard[:, 0 : 2 * S])
+        for cols, home in zip(reversed(pairs), reversed(linear)):
+            nc.vector.scalar_tensor_tensor(
+                out=home, in0=shifted[:, cols], scalar=0.0, in1=bw_sb[:, cols], op0=ALU.min, op1=ALU.subtract
             )
 
-        w_grouped = keep.tile([P, N, PACK], BF16, align_bytes=64, name=f"n2_sb{last}")
+        w_grouped = shifted[:, flat(3)].bitcast(BF16)
         nc.vector.tensor_copy(
-            out=w_grouped[:].rearrange("p (c i) j -> p c j i", i=4),
-            in_=w_raw[:].rearrange("p j (c i) -> p c j i", i=4),
+            out=w_grouped.rearrange("p (c i j) -> p c j i", i=4, j=PACK),
+            in_=w_signed[:].rearrange("p j (c i) -> p c j i", i=4),
         )
-        bw_plus = keep.tile([P, PACK * S], F32)
-        w_codes = keep.tile([P, N], U32, align_bytes=64)
         w_bytes = keep.tile([P, N], U8, align_bytes=64)
-        for u in range(2):
-            cols = slice(2 * u * S, 2 * (u + 1) * S)
-            nc.vector.scalar_tensor_tensor(
-                out=bw_plus[:, cols], in0=z_high[:, cols], scalar=LINEAR_FROM, in1=bw_sb[:, cols],
-                op0=ALU.subtract, op1=ALU.add,
-            )
-        nc.vector.quantize_mx(
-            out=w_codes[:].bitcast(FP8X4), scales=w_bytes[:], in_=w_grouped[:].rearrange("p c j -> p (c j)")
-        )
         loo_gain = keep.tile([P, PACK], F32)
-        nc.gpsimd.tensor_scalar(out=loo_gain[:], in0=unit_sb[:], scalar1=-0.6, scalar2=0.0, op0=ALU.mult, op1=ALU.add)
-        tiny = keep.tile([P, 1], F32)
-        nc.gpsimd.memset(tiny[:], TINY)
+        nc.vector.tensor_scalar(
+            out=loo_gain[:], in0=unit_size[:], scalar1=LOO_WEIGHT * MEAN_SHIFT, scalar2=FLOOR, op0=ALU.mult, op1=ALU.max
+        )
 
-        log_home = {first: z_yard[:, 0:S], second: z_yard[:, S : 2 * S], third: sig[first], last: sig[second]}
-        den = [keep.tile([P, S], F32, name=f"den{t}") for t in range(PACK)]
-        den_sq = [keep.tile([P, S], F32, name=f"den_sq{t}") for t in range(2)] * 2
-        for t in ORDER:
-            nc.scalar.activation(out=log_home[t], in_=sig[t], func=ACT.Ln, bias=tiny[:])
+        spans = (slice(0, cut), slice(cut, 2 * S))
+        early_logs = [
+            keep.tile([P, cut], F32, name="first_logs", tag="first_logs", align_bytes=64),
+            keep.tile([P, 2 * S - cut], F32, name="second_logs"),
+        ]
+        den = keep.tile([P, PACK * S], F32)
+        den_sq = keep.tile([P, PACK * S], F32)
+        for cols, logs in zip(spans, early_logs):
+            nc.scalar.activation(out=logs[:], in_=sig[:, cols], func=ACT.Ln, bias=tiny[:])
+        late_logs = {2: sig_yard[:, 0:S], 3: sig[:, flat(1)]}
+        for t in late_logs:
+            nc.scalar.activation(out=late_logs[t], in_=sig[:, flat(t)], func=ACT.Ln, bias=tiny[:])
+
+        def denominator(cols, log_values, linear_values):
             nc.vector.scalar_tensor_tensor(
-                out=den[t][:], in0=log_home[t], scalar=-LINEAR_FROM, in1=bw_plus[:, t * S : (t + 1) * S],
-                op0=ALU.max, op1=ALU.subtract,
+                out=den[:, cols], in0=log_values, scalar=-LINEAR_FROM, in1=linear_values, op0=ALU.max, op1=ALU.add
             )
-            if t < 2:
-                nc.vector.tensor_tensor(out=den_sq[t][:], in0=den[t][:], in1=den[t][:], op=ALU.mult)
 
-        ker = [keep.tile([P, S], F32, name=f"ker{t}") for t in range(PACK)]
-        ker_sib = [keep.tile([P, S], F32, name=f"ker_sib{t}") for t in range(PACK)]
-        loo = [keep.tile([P, S], F32, name=f"loo{t}") for t in range(PACK)]
-        penalty = [keep.tile([P, S], F32, name=f"penalty{t}") for t in range(PACK)]
+        def den_square(cols):
+            nc.vector.tensor_tensor(out=den_sq[:, cols], in0=den[:, cols], in1=den[:, cols], op=ALU.mult)
+
+        def scalar_den_square(cols):
+            nc.scalar.activation(out=den_sq[:, cols], in_=den[:, cols], func=ACT.Square)
+
+        denominator(spans[0], early_logs[0][:], linear[0][:, spans[0]])
+        w_codes = keep.tile([P, N], U32, name="w_codes", tag="first_logs", align_bytes=64)
+        nc.vector.quantize_mx(out=w_codes[:].bitcast(FP8X4), scales=w_bytes[:], in_=w_grouped)
+        denominator(spans[1], early_logs[1][:], linear[0][:, spans[1]])
+        denominator(flat(2), late_logs[2], linear[1][:, flat(0)])
+        den_square(flat(0))
+        denominator(flat(3), late_logs[3], linear[1][:, flat(1)])
+        den_square(flat(1))
+
+        ker = keep.tile([P, PACK, S], F32)
         row_sum = keep.tile([P, PACK], F32)
+        mean_plus = keep.tile([P, PACK], F32)
+        inverse_mean = keep.tile([P, PACK], F32)
         ker_gain = keep.tile([P, PACK], F32)
-        hid = [keep.tile([P, PACK, HALF], BF16, name=f"hid{h}") for h in range(2)]
-        inv_home = {first: sig_yard[:, 0:S], second: sig_yard[:, S : 2 * S], third: den[first][:], last: den[second][:]}
+        inverse = [sig[:, 3 * S - HALF : 4 * S - HALF], shifted[:, flat(0)], shifted[:, flat(1)], shifted[:, flat(2)]]
+        inverse_root = sig[:, 4 * S - PACK :]
+        nc.scalar.activation(out=inverse_root, in_=loo_gain[:], func=ACT.Abs_reciprocal_sqrt)
+        root = keep.tile([P, PACK], F32)
+
+        def make_root():
+            nc.vector.tensor_tensor(out=root[:], in0=inverse_root, in1=loo_gain[:], op=ALU.mult)
+
         out_rows = out.rearrange("(b p) c -> p b c", p=P)
-        weighted = {t: keep.tile([P, S], F32, name=f"weighted{t}") for t in ORDER[2:]}
+        widths = [cols.stop - cols.start for cols in CHUNKS]
+        halves = {
+            name: [keep.tile([P, PACK, HALF], dtype, name=f"{name}{h}") for h in range(2)]
+            for name, dtype in (("ker_sib", F32), ("loo", F32), ("penalty", F32), ("hid", BF16))
+        }
 
-        def reciprocal_row(t):
-            nc.scalar.activation(out=inv_home[t], in_=den_sq[t][:], func=ACT.Abs_reciprocal_sqrt)
+        def part(name, rows, cols):
+            h, lo = divmod(cols.start, HALF)
+            return halves[name][h][:, rows, lo : lo + cols.stop - cols.start]
 
-        def vector_den_square(t):
-            nc.vector.tensor_tensor(out=den_sq[t][:], in0=den[t][:], in1=den[t][:], op=ALU.mult)
-
-        def scalar_den_square(t):
-            nc.scalar.activation(out=den_sq[t][:], in_=den[t][:], func=ACT.Square)
+        def reciprocal_row(t, cols=whole):
+            nc.scalar.activation(out=inverse[t][:, cols], in_=den_sq[:, flat(t, cols)], func=ACT.Abs_reciprocal_sqrt)
 
         def kernel_row(t):
             nc.vector.scalar_tensor_tensor(
-                out=ker[t][:], in0=inv_home[t], scalar=1.0, in1=bw_sb[:, t * S : (t + 1) * S],
+                out=ker[:, t, :], in0=inverse[t], scalar=root[:, t : t + 1], in1=bw_sb[:, flat(t)],
                 op0=ALU.mult, op1=ALU.mult, accum_out=row_sum[:, t : t + 1],
             )
 
-        def gains(cols):
-            width = cols.stop - cols.start
-            shifted = ring.tile([P, width], F32)
-            nc.vector.tensor_scalar(
-                out=shifted[:], in0=row_sum[:, cols], scalar1=1.0 / S, scalar2=0.2, op0=ALU.mult, op1=ALU.add
-            )
-            inverse = ring.tile([P, width], F32)
-            nc.vector.reciprocal(out=inverse[:], in_=shifted[:])
-            nc.vector.tensor_tensor(out=ker_gain[:, cols], in0=inverse[:], in1=unit_sb[:, cols], op=ALU.mult)
-
-        def fetch(t, cols):
-            entries = slice(cols.start // LIST_GROUP, cols.stop // LIST_GROUP)
-            nc.scalar.activation(out=ker_sib[t][:, cols], in_=ker[t][:].indirect(sib_sb[:, entries]), func=ACT.Copy)
-
-        def difference(t, cols):
-            nc.vector.tensor_tensor(out=loo[t][:, cols], in0=ker[t][:, cols], in1=ker_sib[t][:, cols], op=ALU.subtract)
-
-        def weigh(t):
-            nc.scalar.activation(out=weighted[t][:], in_=ker[t][:], func=ACT.Copy, scale=ker_gain[:, t : t + 1])
-
-        def square(t, cols):
-            if t in weighted:
-                nc.scalar.activation(out=penalty[t][:, cols], in_=loo[t][:, cols], func=ACT.Square)
-            else:
-                nc.vector.scalar_tensor_tensor(
-                    out=penalty[t][:, cols], in0=loo[t][:, cols], scalar=loo_gain[:, t : t + 1], in1=loo[t][:, cols],
-                    op0=ALU.mult, op1=ALU.mult,
-                )
-
-        def hidden(t, cols):
-            h, lo = divmod(cols.start, HALF)
-            if t in weighted:
-                scaled, gain, plain = penalty[t], loo_gain, weighted[t]
-            else:
-                scaled, gain, plain = ker[t], ker_gain, penalty[t]
+        def shift_mean(rows):
             nc.vector.scalar_tensor_tensor(
-                out=hid[h][:, t, lo : lo + cols.stop - cols.start], in0=scaled[:, cols], scalar=gain[:, t : t + 1], in1=plain[:, cols],
+                out=mean_plus[:, rows], in0=row_sum[:, rows], scalar=1.0 / (S * MEAN_SHIFT), in1=root[:, rows],
                 op0=ALU.mult, op1=ALU.add,
             )
 
-        def readout(n, group_copy, out_copy):
-            cols = CHUNKS[n]
-            width = cols.stop - cols.start
-            h, lo = divmod(cols.start, HALF)
-            hid_grouped = keep.tile([P, width, PACK], BF16, align_bytes=64, name=f"hid_grouped{n}")
-            group_copy(
-                out=hid_grouped[:].rearrange("p (c i) t -> p c t i", i=4),
-                in_=hid[h][:, :, lo : lo + width].rearrange("p t (c i) -> p c t i", i=4),
+        def invert_mean(rows):
+            nc.vector.reciprocal(out=inverse_mean[:, rows], in_=mean_plus[:, rows])
+
+        def gain(rows):
+            nc.vector.tensor_tensor(out=ker_gain[:, rows], in0=inverse_mean[:, rows], in1=unit_size[:, rows], op=ALU.mult)
+
+        def fetch(t, cols):
+            entries = slice(cols.start // LIST_GROUP, cols.stop // LIST_GROUP)
+            nc.scalar.activation(out=part("ker_sib", t, cols), in_=ker[:, t, :].indirect(sib_sb[:, entries]), func=ACT.Copy)
+
+        def difference(rows, cols):
+            nc.vector.tensor_tensor(out=part("loo", rows, cols), in0=ker[:, rows, cols], in1=part("ker_sib", rows, cols), op=ALU.subtract)
+
+        def scalar_square(rows, cols):
+            nc.scalar.activation(out=part("penalty", rows, cols), in_=part("loo", rows, cols), func=ACT.Square)
+
+        def vector_square(rows, cols):
+            nc.vector.tensor_tensor(out=part("penalty", rows, cols), in0=part("loo", rows, cols), in1=part("loo", rows, cols), op=ALU.mult)
+
+        def hidden(t, cols):
+            nc.vector.scalar_tensor_tensor(
+                out=part("hid", t, cols), in0=ker[:, t, cols], scalar=ker_gain[:, t : t + 1], in1=part("penalty", t, cols),
+                op0=ALU.mult, op1=ALU.subtract,
             )
+
+        hid_grouped = [keep.tile([P, w, PACK], BF16, align_bytes=64, name=f"hid_grouped{n}") for n, w in enumerate(widths)]
+
+        def interleave(n, copy):
+            copy(
+                out=hid_grouped[n][:].rearrange("p (c i) t -> p c t i", i=4),
+                in_=part("hid", slice(0, PACK), CHUNKS[n]).rearrange("p t (c i) -> p c t i", i=4),
+            )
+
+        def readout(n, copies):
+            cols, width = CHUNKS[n], widths[n]
             hid_codes = keep.tile([P, width], U32, align_bytes=64, name=f"hid_codes{n}")
             hid_bytes = keep.tile([P, width], U8, align_bytes=64, name=f"hid_bytes{n}")
             nc.vector.quantize_mx(
                 out=hid_codes[:].bitcast(FP8X4), scales=hid_bytes[:],
-                in_=hid_grouped[:].rearrange("p c t -> p (c t)"),
+                in_=hid_grouped[n][:].rearrange("p c t -> p (c t)"),
             )
-            acc = psum.tile([P, N // P, width], F32, name=f"acc{n}")
-            for b in range(N // P):
-                nc.tensor.matmul_mx(
-                    out=acc[:, b, :],
-                    lhsT=w_codes[:, b * P : (b + 1) * P].bitcast(FP8X4),
-                    lhsT_scale=w_bytes[:, b * P : (b + 1) * P],
-                    rhs=hid_codes[:].bitcast(FP8X4),
-                    rhs_scale=hid_bytes[:],
-                    start=True,
-                    stop=True,
-                )
             result = keep.tile([P, N // P, width], F32, name=f"result{n}")
-            out_copy(out=result[:], in_=acc[:])
+            groups = [slice(0, 2)] if len(copies) == 1 else [slice(0, 1), slice(1, 2)]
+            for g, (blocks, copy) in enumerate(zip(groups, copies)):
+                acc = psum.tile([P, blocks.stop - blocks.start, width], F32, name=f"acc{n}{g}", tag=f"bank{2 * n + g}")
+                for b in range(blocks.start, blocks.stop):
+                    nc.tensor.matmul_mx(
+                        out=acc[:, b - blocks.start, :],
+                        lhsT=w_codes[:, b * P : (b + 1) * P].bitcast(FP8X4),
+                        lhsT_scale=w_bytes[:, b * P : (b + 1) * P],
+                        rhs=hid_codes[:].bitcast(FP8X4),
+                        rhs_scale=hid_bytes[:],
+                        start=True,
+                        stop=True,
+                    )
+                copy(out=result[:, blocks, :], in_=acc[:])
             nc.sync.dma_start(out=out_rows[:, :, cols], in_=result[:])
 
-        whole = slice(0, S)
-        left, right = HALVES
-        reciprocal_row(first)
-        reciprocal_row(second)
-        kernel_row(first)
-        fetch(first, left)
-        kernel_row(second)
-        vector_den_square(third)
-        fetch(first, right)
-        reciprocal_row(third)
-        scalar_den_square(last)
-        difference(first, whole)
-        kernel_row(third)
-        fetch(second, left)
-        reciprocal_row(last)
-        fetch(second, right)
-        square(first, whole)
-        kernel_row(last)
-        difference(second, whole)
-        for t in (third, last):
-            for cols in HALVES:
-                fetch(t, cols)
-        gains(slice(first, last + 1))
-        square(second, whole)
-        difference(third, whole)
-        difference(last, whole)
-        for t in weighted:
-            weigh(t)
-        for cols in HALVES:
-            for t in (third, last):
-                square(t, cols)
-        for t in (first, second):
-            for cols in HALVES:
-                hidden(t, cols)
-        for t in (third, last):
-            hidden(t, left)
-        readout(0, nc.vector.tensor_copy, nc.scalar.copy)
-        hidden(third, right)
-        for cols in CHUNKS[1:]:
-            hidden(last, cols)
-        for n in range(1, len(CHUNKS)):
-            readout(n, (nc.scalar.copy, nc.vector.tensor_copy)[n - 1], (nc.scalar.copy, nc.vector.tensor_copy)[n - 1])
+        everything = slice(0, PACK)
+        r0, r1, r2, r3 = (slice(t, t + 1) for t in range(PACK))
+        reciprocal_row(0)
+        reciprocal_row(1)
+        make_root()
+        den_square(flat(2))
+        kernel_row(0)
+        reciprocal_row(2)
+        scalar_den_square(flat(3))
+        kernel_row(1)
+        reciprocal_row(3)
+        fetch(0, left)
+        kernel_row(2)
+        fetch(1, left)
+        difference(r0, left)
+        kernel_row(3)
+        fetch(2, left)
+        fetch(3, left)
+        difference(r1, left)
+        shift_mean(everything)
+        vector_square(EARLY, left)
+        invert_mean(everything)
+        difference(r2, left)
+        gain(everything)
+        difference(r3, left)
+        for t in range(PACK):
+            fetch(t, right)
+        hidden(0, left)
+        hidden(1, left)
+        difference(EARLY, right)
+        scalar_square(LATE, left)
+        difference(LATE, right)
+        hidden(2, left)
+        hidden(3, left)
+        scalar_square(EARLY, right)
+        scalar_square(LATE, right)
+        interleave(0, nc.scalar.copy)
+        hidden(0, right)
+        hidden(1, right)
+        readout(0, [nc.scalar.copy])
+        for n in (1, 2):
+            for t in (2, 3):
+                hidden(t, CHUNKS[n])
+        interleave(1, nc.vector.tensor_copy)
+        interleave(2, nc.vector.tensor_copy)
+        readout(1, [nc.scalar.copy])
+        readout(2, [nc.vector.tensor_copy, nc.scalar.copy])

@@ -56,12 +56,12 @@ def tile_picked_ylandk_sqr_p_kernel(
         h_raw = [keep.tile([P, PACK, H // 2], F32, name=f"h_raw{u}") for u in range(2)]
         for u in range(2):
             nc.sync.dma_start(out=h_raw[u][:], in_=h_rows[:, :, u * (H // 2) : (u + 1) * (H // 2)])
-        nc.sync.dma_start(out=unit_sb[:], in_=unit.rearrange("(p t) o -> p (t o)", t=PACK))
         n2_rows = n2.rearrange("(p t) c -> p (t c)", t=PACK)
         n2_yard = keep.tile([P, 2 * S - HALF + PACK * S], F32)
         n2_sb = n2_yard[:, 2 * S - HALF :]
         w_raw = keep.tile([P, PACK, N], F32)
         nc.sync.dma_start(out=w_raw[:], in_=w1.rearrange("(p j) m -> p j m", j=PACK))
+        nc.sync.dma_start(out=unit_sb[:], in_=unit.rearrange("(p t) o -> p (t o)", t=PACK))
         for t in (1, 2, 3, 0):
             nc.sync.dma_start(out=n2_sb[:, flat(t)], in_=n2_rows[:, flat(t)])
         bw_rows = bw.rearrange("(p t) c -> p (t c)", t=PACK)
@@ -113,7 +113,7 @@ def tile_picked_ylandk_sqr_p_kernel(
                 scales=h_bytes[:, t, :],
                 in_=h_grouped[:, t, :, :].rearrange("p m j -> p (m j)"),
             )
-        pieces = ((1, left), (1, right), (2, whole), (3, whole), (0, left), (0, right))
+        pieces = [(t, cols) for t in (1, 2, 3, 0) for cols in (left, right)]
         for bank, (t, cols) in enumerate(pieces):
             y = psum.tile([P, cols.stop - cols.start], F32, name=f"y{bank}", tag=f"bank{bank}")
             nc.tensor.matmul_mx(
@@ -247,10 +247,12 @@ def tile_picked_ylandk_sqr_p_kernel(
 
         hid_grouped = [keep.tile([P, w, PACK], BF16, align_bytes=64, name=f"hid_grouped{n}") for n, w in enumerate(widths)]
 
-        def interleave(n, copy):
+        def interleave(n, copy, lo=0, hi=None):
+            hi = widths[n] if hi is None else hi
+            cols = slice(CHUNKS[n].start + lo, CHUNKS[n].start + hi)
             copy(
-                out=hid_grouped[n][:].rearrange("p (c i) t -> p c t i", i=4),
-                in_=part("hid", slice(0, PACK), CHUNKS[n]).rearrange("p t (c i) -> p c t i", i=4),
+                out=hid_grouped[n][:, lo:hi, :].rearrange("p (c i) t -> p c t i", i=4),
+                in_=part("hid", slice(0, PACK), cols).rearrange("p t (c i) -> p c t i", i=4),
             )
 
         def readout(n, copies):
@@ -314,14 +316,15 @@ def tile_picked_ylandk_sqr_p_kernel(
         hidden(3, left)
         scalar_square(EARLY, right)
         scalar_square(LATE, right)
-        interleave(0, nc.scalar.copy)
+        interleave(0, nc.scalar.copy, 0, 128)
+        interleave(0, nc.vector.tensor_copy, 128)
         hidden(0, right)
         hidden(1, right)
         readout(0, [nc.scalar.copy])
         for n in (1, 2):
             for t in (2, 3):
                 hidden(t, CHUNKS[n])
-        interleave(1, nc.vector.tensor_copy)
+        interleave(1, nc.scalar.copy)
         interleave(2, nc.vector.tensor_copy)
         readout(1, [nc.scalar.copy])
         readout(2, [nc.vector.tensor_copy, nc.scalar.copy])

from contextlib import ExitStack

import concourse.mybir as mybir

K, T, S, N, H = 512, 1024, 512, 256, 512
FLOPS = 2 * K * H * S + 2 * H * N * S

F32 = mybir.dt.float32
BF16 = mybir.dt.bfloat16
I32 = mybir.dt.int32
U32 = mybir.dt.uint32
U16 = mybir.dt.uint16
U8 = mybir.dt.uint8
FP8X4 = mybir.dt.float8_e4m3fn_x4
ALU = mybir.AluOpType
ACT = mybir.ActivationFunctionType

P = 128
PACK = 4
HALF = S // 2
LIST_GROUP = 16
LINEAR_FROM = 20.0
MEAN_SHIFT = 0.2
LOO_WEIGHT = 0.6
FLOOR = 2.0**-100
SCALAR_SHARE = 24
CHUNKS = (slice(0, 256), slice(256, 384), slice(384, 512))
EARLY, LATE = slice(0, 2), slice(2, 4)


def tile_picked_ylandk_sqr_p_kernel(
    tc, x_words, x_scales, hT, n2, bw, unit, w1, offs, sib, out
):
    nc = tc.nc
    with ExitStack() as ctx:
        keep = ctx.enter_context(tc.tile_pool(name="keep", bufs=1))
        psum = ctx.enter_context(tc.psum_pool(name="psum", bufs=1))

        def flat(t, cols=slice(0, S)):
            return slice(t * S + cols.start, t * S + cols.stop)

        word_table = keep.tile([P, T], I32, align_bytes=64)
        scale_table = keep.tile([P, T], U8, align_bytes=64)
        offs_sb = keep.tile([P, S // LIST_GROUP], U16)
        sib_sb = keep.tile([P, S // LIST_GROUP], U16)
        unit_sb = keep.tile([P, PACK], F32)
        nc.gpsimd.memset(scale_table[:].bitcast(I32), 0)
        nc.sync.dma_start(out=word_table[:], in_=x_words[0].rearrange("p n t -> p (n t)").bitcast(I32))
        for q in range(4):
            nc.sync.dma_start(
                out=scale_table[32 * q : 32 * q + 4, :].bitcast(I32),
                in_=x_scales[0, 4 * q : 4 * q + 4, :].bitcast(I32),
            )
        nc.sync.dma_start(offs_sb[:], offs)
        h_rows = hT.rearrange("(p j) c -> p j c", j=PACK)
        h_raw = [keep.tile([P, PACK, H // 2], F32, name=f"h_raw{u}") for u in range(2)]
        for u in range(2):
            nc.sync.dma_start(out=h_raw[u][:], in_=h_rows[:, :, u * (H // 2) : (u + 1) * (H // 2)])
        n2_rows = n2.rearrange("(p t) c -> p (t c)", t=PACK)
        n2_yard = keep.tile([P, 2 * S - HALF + PACK * S], F32)
        n2_sb = n2_yard[:, 2 * S - HALF :]
        w_raw = keep.tile([P, PACK, N], F32)
        nc.sync.dma_start(out=w_raw[:], in_=w1.rearrange("(p j) m -> p j m", j=PACK))
        nc.sync.dma_start(out=unit_sb[:], in_=unit.rearrange("(p t) o -> p (t o)", t=PACK))
        for t in (1, 2, 3, 0):
            nc.sync.dma_start(out=n2_sb[:, flat(t)], in_=n2_rows[:, flat(t)])
        bw_rows = bw.rearrange("(p t) c -> p (t c)", t=PACK)
        bw_sb = keep.tile([P, PACK * S], F32)
        pairs = (slice(0, 2 * S), slice(2 * S, 4 * S))
        for cols in reversed(pairs):
            nc.sync.dma_start(out=bw_sb[:, cols], in_=bw_rows[:, cols])
        nc.sync.dma_start(sib_sb[:], sib)

        unshift = keep.tile([P, 1], F32)
        nc.gpsimd.memset(unshift[:], -LINEAR_FROM)
        tiny = keep.tile([P, 1], F32)
        nc.scalar.activation(out=tiny[:], in_=unshift[:], func=ACT.Sigmoid, scale=2.0)

        x_codes = keep.tile([P, S], U32, align_bytes=64)
        x_bytes = keep.tile([P, S], U8, align_bytes=64)
        nc.vector.tensor_copy(x_codes[:], word_table[:].bitcast(U32).indirect(offs_sb[:]))
        nc.vector.tensor_copy(x_bytes[:], scale_table[:].indirect(offs_sb[:]))

        h_grouped = keep.tile([P, PACK, P, PACK], BF16, align_bytes=64)
        for u, lo, hi, copy in (
            (0, 0, P // 2, nc.scalar.copy),
            (1, 0, SCALAR_SHARE, nc.scalar.copy),
            (1, SCALAR_SHARE, P // 2, nc.vector.tensor_copy),
        ):
            copy(
                out=h_grouped[:, :, 64 * u + lo : 64 * u + hi, :].rearrange("p t m j -> p m t j"),
                in_=h_raw[u][:, :, PACK * lo : PACK * hi].rearrange("p j (m t) -> p m t j", t=PACK),
            )

        unit_sign = keep.tile([P, PACK], F32)
        nc.scalar.activation(out=unit_sign[:], in_=unit_sb[:], func=ACT.Sign)
        unit_size = keep.tile([P, PACK], F32)
        nc.scalar.activation(out=unit_size[:], in_=unit_sb[:], func=ACT.Abs, scale=1.0 / MEAN_SHIFT)
        w_signed = keep.tile([P, PACK, N], BF16)
        for j in range(PACK):
            nc.scalar.activation(out=w_signed[:, j, :], in_=w_raw[:, j, :], func=ACT.Copy, scale=unit_sign[:, j : j + 1])

        shifted = keep.tile([P, PACK * S], F32, align_bytes=64)
        cut = HALF + HALF // 2
        sig_yard = keep.tile([P, S - cut + PACK * S], F32)
        sig = sig_yard[:, S - cut :]
        left, right, whole = slice(0, HALF), slice(HALF, S), slice(0, S)
        h_codes = keep.tile([P, PACK, P], U32, align_bytes=64)
        h_bytes = keep.tile([P, PACK, P], U8, align_bytes=64)
        for t in (1, 2, 3, 0):
            nc.vector.quantize_mx(
                out=h_codes[:, t, :].bitcast(FP8X4),
                scales=h_bytes[:, t, :],
                in_=h_grouped[:, t, :, :].rearrange("p m j -> p (m j)"),
            )
        pieces = [(t, cols) for t in (1, 2, 3, 0) for cols in (left, right)]
        for bank, (t, cols) in enumerate(pieces):
            y = psum.tile([P, cols.stop - cols.start], F32, name=f"y{bank}", tag=f"bank{bank}")
            nc.tensor.matmul_mx(
                out=y[:],
                lhsT=h_codes[:, t, :].bitcast(FP8X4),
                lhsT_scale=h_bytes[:, t, :],
                rhs=x_codes[:, cols].bitcast(FP8X4),
                rhs_scale=x_bytes[:, cols],
                start=True,
                stop=True,
            )
            at = flat(t, cols)
            nc.vector.scalar_tensor_tensor(
                out=shifted[:, at], in0=y[:], scalar=LINEAR_FROM, in1=n2_sb[:, at], op0=ALU.add, op1=ALU.subtract
            )
            nc.scalar.activation(out=sig[:, at], in_=shifted[:, at], func=ACT.Sigmoid, bias=unshift[:])

        linear = (n2_sb[:, pairs[1]], n2_yard[:, 0 : 2 * S])
        for cols, home in zip(reversed(pairs), reversed(linear)):
            nc.vector.scalar_tensor_tensor(
                out=home, in0=shifted[:, cols], scalar=0.0, in1=bw_sb[:, cols], op0=ALU.min, op1=ALU.subtract
            )

        w_grouped = shifted[:, flat(3)].bitcast(BF16)
        nc.vector.tensor_copy(
            out=w_grouped.rearrange("p (c i j) -> p c j i", i=4, j=PACK),
            in_=w_signed[:].rearrange("p j (c i) -> p c j i", i=4),
        )
        w_bytes = keep.tile([P, N], U8, align_bytes=64)
        loo_gain = keep.tile([P, PACK], F32)
        nc.vector.tensor_scalar(
            out=loo_gain[:], in0=unit_size[:], scalar1=LOO_WEIGHT * MEAN_SHIFT, scalar2=FLOOR, op0=ALU.mult, op1=ALU.max
        )

        spans = (slice(0, cut), slice(cut, 2 * S))
        early_logs = [
            keep.tile([P, cut], F32, name="first_logs", tag="first_logs", align_bytes=64),
            keep.tile([P, 2 * S - cut], F32, name="second_logs"),
        ]
        den = keep.tile([P, PACK * S], F32)
        den_sq = keep.tile([P, PACK * S], F32)
        for cols, logs in zip(spans, early_logs):
            nc.scalar.activation(out=logs[:], in_=sig[:, cols], func=ACT.Ln, bias=tiny[:])
        late_logs = {2: sig_yard[:, 0:S], 3: sig[:, flat(1)]}
        for t in late_logs:
            nc.scalar.activation(out=late_logs[t], in_=sig[:, flat(t)], func=ACT.Ln, bias=tiny[:])

        def denominator(cols, log_values, linear_values):
            nc.vector.scalar_tensor_tensor(
                out=den[:, cols], in0=log_values, scalar=-LINEAR_FROM, in1=linear_values, op0=ALU.max, op1=ALU.add
            )

        def den_square(cols):
            nc.vector.tensor_tensor(out=den_sq[:, cols], in0=den[:, cols], in1=den[:, cols], op=ALU.mult)

        def scalar_den_square(cols):
            nc.scalar.activation(out=den_sq[:, cols], in_=den[:, cols], func=ACT.Square)

        denominator(spans[0], early_logs[0][:], linear[0][:, spans[0]])
        w_codes = keep.tile([P, N], U32, name="w_codes", tag="first_logs", align_bytes=64)
        nc.vector.quantize_mx(out=w_codes[:].bitcast(FP8X4), scales=w_bytes[:], in_=w_grouped)
        denominator(spans[1], early_logs[1][:], linear[0][:, spans[1]])
        denominator(flat(2), late_logs[2], linear[1][:, flat(0)])
        den_square(flat(0))
        denominator(flat(3), late_logs[3], linear[1][:, flat(1)])
        den_square(flat(1))

        ker = keep.tile([P, PACK, S], F32)
        row_sum = keep.tile([P, PACK], F32)
        mean_plus = keep.tile([P, PACK], F32)
        inverse_mean = keep.tile([P, PACK], F32)
        ker_gain = keep.tile([P, PACK], F32)
        inverse = [sig[:, 3 * S - HALF : 4 * S - HALF], shifted[:, flat(0)], shifted[:, flat(1)], shifted[:, flat(2)]]
        inverse_root = sig[:, 4 * S - PACK :]
        nc.scalar.activation(out=inverse_root, in_=loo_gain[:], func=ACT.Abs_reciprocal_sqrt)
        root = keep.tile([P, PACK], F32)

        def make_root():
            nc.vector.tensor_tensor(out=root[:], in0=inverse_root, in1=loo_gain[:], op=ALU.mult)

        out_rows = out.rearrange("(b p) c -> p b c", p=P)
        widths = [cols.stop - cols.start for cols in CHUNKS]
        halves = {
            name: [keep.tile([P, PACK, HALF], dtype, name=f"{name}{h}") for h in range(2)]
            for name, dtype in (("ker_sib", F32), ("loo", F32), ("penalty", F32), ("hid", BF16))
        }

        def part(name, rows, cols):
            h, lo = divmod(cols.start, HALF)
            return halves[name][h][:, rows, lo : lo + cols.stop - cols.start]

        def reciprocal_row(t, cols=whole):
            nc.scalar.activation(out=inverse[t][:, cols], in_=den_sq[:, flat(t, cols)], func=ACT.Abs_reciprocal_sqrt)

        def kernel_row(t):
            nc.vector.scalar_tensor_tensor(
                out=ker[:, t, :], in0=inverse[t], scalar=root[:, t : t + 1], in1=bw_sb[:, flat(t)],
                op0=ALU.mult, op1=ALU.mult, accum_out=row_sum[:, t : t + 1],
            )

        def shift_mean(rows):
            nc.vector.scalar_tensor_tensor(
                out=mean_plus[:, rows], in0=row_sum[:, rows], scalar=1.0 / (S * MEAN_SHIFT), in1=root[:, rows],
                op0=ALU.mult, op1=ALU.add,
            )

        def invert_mean(rows):
            nc.vector.reciprocal(out=inverse_mean[:, rows], in_=mean_plus[:, rows])

        def gain(rows):
            nc.vector.tensor_tensor(out=ker_gain[:, rows], in0=inverse_mean[:, rows], in1=unit_size[:, rows], op=ALU.mult)

        def fetch(t, cols):
            entries = slice(cols.start // LIST_GROUP, cols.stop // LIST_GROUP)
            nc.scalar.activation(out=part("ker_sib", t, cols), in_=ker[:, t, :].indirect(sib_sb[:, entries]), func=ACT.Copy)

        def difference(rows, cols):
            nc.vector.tensor_tensor(out=part("loo", rows, cols), in0=ker[:, rows, cols], in1=part("ker_sib", rows, cols), op=ALU.subtract)

        def scalar_square(rows, cols):
            nc.scalar.activation(out=part("penalty", rows, cols), in_=part("loo", rows, cols), func=ACT.Square)

        def vector_square(rows, cols):
            nc.vector.tensor_tensor(out=part("penalty", rows, cols), in0=part("loo", rows, cols), in1=part("loo", rows, cols), op=ALU.mult)

        def hidden(t, cols):
            nc.vector.scalar_tensor_tensor(
                out=part("hid", t, cols), in0=ker[:, t, cols], scalar=ker_gain[:, t : t + 1], in1=part("penalty", t, cols),
                op0=ALU.mult, op1=ALU.subtract,
            )

        hid_grouped = [keep.tile([P, w, PACK], BF16, align_bytes=64, name=f"hid_grouped{n}") for n, w in enumerate(widths)]

        def interleave(n, copy, lo=0, hi=None):
            hi = widths[n] if hi is None else hi
            cols = slice(CHUNKS[n].start + lo, CHUNKS[n].start + hi)
            copy(
                out=hid_grouped[n][:, lo:hi, :].rearrange("p (c i) t -> p c t i", i=4),
                in_=part("hid", slice(0, PACK), cols).rearrange("p t (c i) -> p c t i", i=4),
            )

        def readout(n, copies):
            cols, width = CHUNKS[n], widths[n]
            hid_codes = keep.tile([P, width], U32, align_bytes=64, name=f"hid_codes{n}")
            hid_bytes = keep.tile([P, width], U8, align_bytes=64, name=f"hid_bytes{n}")
            nc.vector.quantize_mx(
                out=hid_codes[:].bitcast(FP8X4), scales=hid_bytes[:],
                in_=hid_grouped[n][:].rearrange("p c t -> p (c t)"),
            )
            result = keep.tile([P, N // P, width], F32, name=f"result{n}")
            groups = [slice(0, 2)] if len(copies) == 1 else [slice(0, 1), slice(1, 2)]
            for g, (blocks, copy) in enumerate(zip(groups, copies)):
                acc = psum.tile([P, blocks.stop - blocks.start, width], F32, name=f"acc{n}{g}", tag=f"bank{2 * n + g}")
                for b in range(blocks.start, blocks.stop):
                    nc.tensor.matmul_mx(
                        out=acc[:, b - blocks.start, :],
                        lhsT=w_codes[:, b * P : (b + 1) * P].bitcast(FP8X4),
                        lhsT_scale=w_bytes[:, b * P : (b + 1) * P],
                        rhs=hid_codes[:].bitcast(FP8X4),
                        rhs_scale=hid_bytes[:],
                        start=True,
                        stop=True,
                    )
                copy(out=result[:, blocks, :], in_=acc[:])
            nc.sync.dma_start(out=out_rows[:, :, cols], in_=result[:])

        everything = slice(0, PACK)
        r0, r1, r2, r3 = (slice(t, t + 1) for t in range(PACK))
        reciprocal_row(0)
        reciprocal_row(1)
        make_root()
        den_square(flat(2))
        kernel_row(0)
        reciprocal_row(2)
        scalar_den_square(flat(3))
        kernel_row(1)
        reciprocal_row(3)
        fetch(0, left)
        kernel_row(2)
        fetch(1, left)
        difference(r0, left)
        kernel_row(3)
        fetch(2, left)
        fetch(3, left)
        difference(r1, left)
        shift_mean(everything)
        vector_square(EARLY, left)
        invert_mean(everything)
        difference(r2, left)
        gain(everything)
        difference(r3, left)
        for t in range(PACK):
            fetch(t, right)
        hidden(0, left)
        hidden(1, left)
        difference(EARLY, right)
        scalar_square(LATE, left)
        difference(LATE, right)
        hidden(2, left)
        hidden(3, left)
        scalar_square(EARLY, right)
        scalar_square(LATE, right)
        interleave(0, nc.scalar.copy, 0, 128)
        interleave(0, nc.vector.tensor_copy, 128)
        hidden(0, right)
        hidden(1, right)
        readout(0, [nc.scalar.copy])
        for n in (1, 2):
            for t in (2, 3):
                hidden(t, CHUNKS[n])
        interleave(1, nc.scalar.copy)
        interleave(2, nc.vector.tensor_copy)
        readout(1, [nc.scalar.copy])
        readout(2, [nc.vector.tensor_copy, nc.scalar.copy])
